import numpy as np
import ml_dtypes


def mxq(x, axis, fmt="e4m3"):
    dtype, down = {"e4m3": (ml_dtypes.float8_e4m3fn, 7), "e5m2": (ml_dtypes.float8_e5m2, 14)}[fmt]
    v = np.moveaxis(np.asarray(x, np.float32).astype(ml_dtypes.bfloat16).astype(np.float64), axis, -1)
    blocks = v.reshape(v.shape[:-1] + (-1, 32))
    amax = np.abs(blocks).max(-1, keepdims=True)
    byte = np.maximum(np.where(amax > 0, np.frexp(amax)[1] - 1 + 127, 0) - down, 1)
    scale = np.exp2(byte - 127.0)
    codes = (blocks / scale).astype(np.float32).astype(dtype).astype(np.float64)
    return np.moveaxis((codes * scale).reshape(v.shape), -1, axis)


WIDE = False


def mx_kscale(k):
    if not WIDE:
        return np.ones(k)
    levels = np.array([10, -10, 5, -5, 0])
    if k % 512:
        return np.exp2(np.random.permutation(np.resize(levels, k // 32))).repeat(32)
    a = np.empty((k // 512, 16))
    for p in range(k // 512):
        a[p, :8] = np.random.permutation(np.resize(levels, 8))
        for g in range(8):
            far = levels[np.abs(levels - a[p, g]) >= 10]
            a[p, g + 8] = far[np.random.randint(len(far))]
    return np.exp2(a.ravel()).repeat(32)


def f64(x):
    return np.asarray(x).astype(np.float64)


E2M1 = np.array([0.0, 0.5, 1.0, 1.5, 2.0, 3.0, 4.0, 6.0, -0.0, -0.5, -1.0, -1.5, -2.0, -3.0, -4.0, -6.0])


def pack_weight(w, fmt):
    k, n = w.shape
    w = f64(np.asarray(w, np.float32).astype(ml_dtypes.bfloat16)).reshape(k // 32, 32, n)
    amax = np.abs(w).max(1)
    if fmt == "e4m3":
        byte = np.frexp(amax)[1] - 1 + 127 - 7
    else:
        mant, ex = np.frexp(amax / 6.0)
        byte = np.where(mant > 0.5, ex, ex - 1) + 127
    byte = np.clip(np.where(amax > 0, byte, 1), 1, 254)
    scaled = (w * np.exp2(127.0 - byte)[:, None, :]).reshape(k, n).astype(np.float32)
    by_word = np.ascontiguousarray(scaled.reshape(k // 512, 128, 4, n).transpose(0, 1, 3, 2))
    if fmt == "e4m3":
        words = by_word.astype(ml_dtypes.float8_e4m3fn).view(np.uint8)
    else:
        c = by_word.astype(ml_dtypes.float4_e2m1fn).view(np.uint8) & 0xF
        words = (c[..., 0::2] | (c[..., 1::2] << 4)).reshape(k // 512, 128, 2 * n)
    return np.ascontiguousarray(words), np.ascontiguousarray(byte.astype(np.uint8).reshape(k // 512, 16, n))


def unpack_weight(words, scales, fmt):
    g, _, n = scales.shape
    words = np.ascontiguousarray(words).reshape(g, 128, n, -1)
    if fmt == "e4m3":
        vals = words.view(ml_dtypes.float8_e4m3fn).astype(np.float64)
    else:
        nib = np.empty((g, 128, n, 4), np.uint8)
        nib[..., 0::2] = words & 0xF
        nib[..., 1::2] = words >> 4
        vals = E2M1[nib]
    vals = vals * np.repeat(np.exp2(scales.astype(np.float64) - 127.0), 8, axis=1)[..., None]
    return vals.transpose(0, 1, 3, 2).reshape(g * 512, n)


def bf(x):
    return np.asarray(x, np.float32).astype(ml_dtypes.bfloat16)


def planes(Y):
    r, m = Y.shape
    b = f64(bf(Y)).reshape(r // 32, 32, m)
    amax = np.abs(b).max(1)
    byte = np.clip(np.where(amax > 0, np.frexp(amax)[1] - 1 + 127 - 7, 1), 1, 254)
    codes = (b * np.exp2(127.0 - byte)[:, None, :]).reshape(r, m).astype(np.float32).astype(ml_dtypes.float8_e4m3fn).view(np.uint8)
    words = codes.reshape(r // 512, 128, 4, m).transpose(0, 1, 3, 2)
    return np.ascontiguousarray(words), np.ascontiguousarray(byte.astype(np.uint8).reshape(r // 512, 16, m))


K, L, M, T, B, N = 1024, 512, 512, 1024, 128, 512


def setup_inputs():
    n = np.random.standard_normal
    fk = mx_kscale(K)
    fl = mx_kscale(L)
    fm = mx_kscale(M)
    xtp = pack_weight(n((K, T)) / fk[:, None], "e2m1")
    wap = pack_weight(n((K, N)) * 1 / np.sqrt(K) * fk[:, None], "e4m3")
    wqp = pack_weight(n((L, N)) * 1 / np.sqrt(L) * fl[:, None], "e2m1")
    xgp = pack_weight(n((M, B)) / fm[:, None], "e4m3")
    wgp = pack_weight(n((M, N)) * 1 / np.sqrt(M) * fm[:, None], "e4m3")
    return {
        "xt_words": xtp[0],
        "xt_scales": xtp[1],
        "wa_words": wap[0],
        "wa_scales": wap[1],
        "xq": (n((L, T)) / fl[:, None]).astype(np.float32),
        "wq_words": wqp[0],
        "wq_scales": wqp[1],
        "xg_words": xgp[0],
        "xg_scales": xgp[1],
        "wg_words": wgp[0],
        "wg_scales": wgp[1],
    }


def reference(xt_words, xt_scales, wa_words, wa_scales, xq, wq_words, wq_scales, xg_words, xg_scales, wg_words, wg_scales):
    xtu = unpack_weight(xt_words, xt_scales, "e2m1")
    wau = unpack_weight(wa_words, wa_scales, "e4m3")
    wqu = unpack_weight(wq_words, wq_scales, "e2m1")
    xgu = unpack_weight(xg_words, xg_scales, "e4m3")
    wgu = unpack_weight(wg_words, wg_scales, "e4m3")
    xqq = mxq(f64(xq), 0, "e4m3")
    z = wau.T @ xtu + wqu.T @ xqq
    u = z.reshape(N, B, T // B).max(axis=2)
    g = wgu.T @ xgu
    y = u - np.mean(z, axis=1, keepdims=True) + 0.5 * g
    words, scales = planes(y)
    return y, words, scales

@@ -1,0 +1,255 @@
+from contextlib import ExitStack
+
+import concourse.mybir as mybir
+from concourse.masks import make_identity
+
+K, L, M, T, B, N = 1024, 512, 512, 1024, 128, 512
+FLOPS = 2 * N * (K * T + L * T + M * B)
+
+F32 = mybir.dt.float32
+BF16 = mybir.dt.bfloat16
+I32 = mybir.dt.int32
+U8 = mybir.dt.uint8
+FP8X4 = mybir.dt.float8_e4m3fn_x4
+FP4X4 = mybir.dt.float4_e2m1fn_x4
+ALU = mybir.AluOpType
+ACT = mybir.ActivationFunctionType
+
+P = 128
+HALF = 512
+QUARTER = 256
+UNIT = 128
+GROUP = 8
+
+
+def tile_mix_peak_of_mixed_sum_pl_kernel(tc, xt_words, xt_scales, wa_words, wa_scales, xq, wq_words, wq_scales,
+                                              xg_words, xg_scales, wg_words, wg_scales, out_0, out_1, out_2):
+    nc = tc.nc
+    with ExitStack() as ctx:
+        keep = ctx.enter_context(tc.tile_pool(name="keep", bufs=1))
+        stage = ctx.enter_context(tc.tile_pool(name="stage", bufs=3))
+        junk = ctx.enter_context(tc.tile_pool(name="junk", bufs=2))
+        psum = ctx.enter_context(tc.psum_pool(name="psum", bufs=1))
+        ctx.enter_context(tc.manual_schedule())
+
+        def sb(name, shape, dtype):
+            return keep.tile(shape, dtype, name=name, align_bytes=64)
+
+        def load_scales(queue, plane, scales, quads=range(4)):
+            for q in quads:
+                queue.dma_start(
+                    out=plane[32 * q:32 * q + 4, :].bitcast(I32).rearrange("r (z c) -> r z c", z=scales.shape[0]),
+                    in_=scales[:, 4 * q:4 * q + 4, :].rearrange("z r c -> r z c").bitcast(I32))
+
+        def deal_scales(dst, raw):
+            nc.vector.tensor_copy(out=dst[:].rearrange("p (z r a i) -> p z a r i", r=4, a=8, i=16),
+                                  in_=raw[:].rearrange("p (z a i r) -> p z a r i", r=4, a=8, i=16))
+
+        was_raw = sb("was_raw", [P, 2 * N], U8)
+        wqs_raw = sb("wqs_raw", [P, N], U8)
+        xts = sb("xts", [P, 2 * T], U8)
+        wgs = sb("wgs", [P, N], U8)
+        xgs = sb("xgs", [P, B], U8)
+        ident = sb("ident", [P, P], F32)
+
+        nc.vector.memset(was_raw[:].bitcast(I32), 0)
+        nc.vector.memset(wqs_raw[:].bitcast(I32), 0)
+        nc.vector.memset(wgs[:].bitcast(I32), 0)
+        nc.vector.memset(xgs[:].bitcast(I32), 0)
+        warm = sb("warm", [P, 8], F32)
+        warm2 = sb("warm2", [P, 8], F32)
+        nc.vector.memset(warm[:], 0.0)
+        nc.scalar.activation(out=warm2[:], in_=warm[:], func=ACT.Identity)
+        load_scales(nc.gpsimd, wqs_raw, wq_scales, (1,))
+        nc.gpsimd.memset(xts[:].bitcast(I32), 0)
+        load_scales(nc.gpsimd, wqs_raw, wq_scales, (2, 3))
+        make_identity(nc, ident[:])
+
+        def load_quarter(c):
+            raw = stage.tile([P, 4, QUARTER], F32, name="raw%d" % c, tag="stage", align_bytes=64)
+            nc.sync.dma_start(out=raw[:], in_=xq[:, c * QUARTER:(c + 1) * QUARTER].rearrange("(p j) t -> p j t", j=4))
+            return raw
+
+        def load_xt(h):
+            words = sb("xt%d" % h, [P, 2, 2 * HALF], U8)
+            nc.sync.dma_start(out=words[:].bitcast(I32),
+                              in_=xt_words[:, :, 2 * h * HALF:2 * (h + 1) * HALF].rearrange("z p c -> p z c").bitcast(I32))
+            return words
+
+        wa_raw = stage.tile([P, 2, N], I32, name="wa_raw", tag="stage", align_bytes=64)
+        nc.sync.dma_start(out=wa_raw[:], in_=wa_words.rearrange("z p n t -> p z (n t)").bitcast(I32))
+        load_scales(nc.sync, was_raw, wa_scales)
+        xt = [load_xt(0)]
+        raw = [load_quarter(0), load_quarter(1)]
+
+        wq_raw = sb("wq_raw", [P, 2 * N], U8)
+        load_scales(nc.scalar, xts, xt_scales)
+        nc.scalar.dma_start(out=wq_raw[:].bitcast(I32), in_=wq_words[0].bitcast(I32))
+        load_scales(nc.scalar, wqs_raw, wq_scales, (0,))
+        load_scales(nc.gpsimd, xgs, xg_scales)
+
+        wa = [sb("wa%d" % z, [P, N], I32) for z in range(2)]
+        was = sb("was", [P, 2 * N], U8)
+        wq = sb("wq", [P, 2 * N], U8)
+        wqs = sb("wqs", [P, N], U8)
+
+        def deal_wa(z):
+            nc.vector.tensor_copy(out=wa[z][:].rearrange("p (r a i) -> p a r i", r=4, i=4),
+                                  in_=wa_raw[:, z, :].rearrange("p (a i r) -> p a r i", r=4, i=4))
+
+        deal_wa(0)
+        deal_wa(1)
+        deal_scales(was, was_raw)
+
+        raw.append(load_quarter(2))
+        xt.append(load_xt(1))
+
+        codes = [sb("xq_codes%d" % h, [P, HALF], I32) for h in range(2)]
+        planes = [sb("xq_plane%d" % h, [P, HALF], U8) for h in range(2)]
+        rounded = [sb("xq_bf%d" % u, [P, 4 * UNIT], BF16) for u in range(T // UNIT)]
+
+        def cast(u):
+            src = raw[u // 2][:, :, (u % 2) * UNIT:(u % 2 + 1) * UNIT].rearrange("p j (c i) -> p c j i", i=4)
+            dst = rounded[u][:].rearrange("p (c i j) -> p c j i", i=4, j=4)
+            if u % 2 == 0:
+                nc.vector.tensor_copy(out=dst, in_=src)
+            else:
+                nc.scalar.copy(out=dst, in_=src)
+
+        def quant(u):
+            h, c = divmod(u, 4)
+            cols = slice(c * UNIT, (c + 1) * UNIT)
+            nc.vector.quantize_mx(out=codes[h][:, cols].bitcast(FP8X4), scales=planes[h][:, cols], in_=rounded[u][:])
+
+        banks = {}
+        for h in range(2):
+            for r in range(4):
+                banks[r, h] = psum.tile([P, HALF], F32, name="z%d%d" % (r, h), tag="bank%d" % (4 * h + r))
+
+        def mm_xt(r, h):
+            for z in range(2):
+                nc.tensor.matmul_mx(out=banks[r, h][:], lhsT=wa[z][:, r * P:(r + 1) * P].bitcast(FP8X4),
+                                    lhsT_scale=was[:, z * N + r * P:z * N + (r + 1) * P],
+                                    rhs=xt[h][:, z, :].bitcast(FP4X4),
+                                    rhs_scale=xts[:, z * T + h * HALF:z * T + (h + 1) * HALF],
+                                    start=(z == 0), stop=False)
+
+        def mm_xq(r, h):
+            nc.tensor.matmul_mx(out=banks[r, h][:], lhsT=wq[:, 2 * r * P:2 * (r + 1) * P].bitcast(FP4X4),
+                                lhsT_scale=wqs[:, r * P:(r + 1) * P],
+                                rhs=codes[h][:].bitcast(FP8X4), rhs_scale=planes[h][:], start=False, stop=True)
+
+        peak = sb("peak", [P, 4, B], F32)
+        part = sb("part", [P, 4], F32)
+        negmean = sb("negmean", [P, 4], F32)
+        y = sb("y", [P, 4, B], F32)
+
+        def take_peak(r, h):
+            nc.vector.tensor_reduce(out=peak[:, r, h * 64:(h + 1) * 64],
+                                    in_=banks[r, h][:].rearrange("p (b j) -> p b j", j=GROUP),
+                                    axis=mybir.AxisListType.X, op=ALU.max)
+
+        def take_sum(r, h):
+            spill = junk.tile([P, HALF], BF16, name="spill")
+            if h == 0:
+                nc.scalar.activation(out=spill[:], in_=banks[r, h][:], func=ACT.Identity, scale=-1.0 / (T * HALF),
+                                     accum_out=part[:, r:r + 1])
+            else:
+                nc.scalar.activation(out=spill[:], in_=banks[r, h][:], func=ACT.Identity, scale=-1.0 / T,
+                                     bias=part[:, r:r + 1], accum_out=negmean[:, r:r + 1])
+
+        for r in range(3):
+            mm_xt(r, 0)
+
+        cast(0)
+        cast(1)
+        nc.vector.tensor_copy(out=wq[:].rearrange("p (r a i e) -> p a r i e", r=4, i=8, e=2),
+                              in_=wq_raw[:].rearrange("p (a i r e) -> p a r i e", r=4, i=8, e=2))
+        quant(0)
+        quant(1)
+
+        raw.append(load_quarter(3))
+        wg = sb("wg", [P, N], I32)
+        xg = sb("xg", [P, B], I32)
+        nc.sync.dma_start(out=wg[:], in_=wg_words[0].rearrange("p n t -> p (n t)").bitcast(I32))
+        nc.sync.dma_start(out=xg[:], in_=xg_words[0].rearrange("p n t -> p (n t)").bitcast(I32))
+        load_scales(nc.sync, wgs, wg_scales)
+
+        cast(2)
+        cast(3)
+        deal_scales(wqs, wqs_raw)
+        quant(2)
+        quant(3)
+
+        mm_xq(0, 0)
+        mm_xq(1, 0)
+        mm_xt(3, 0)
+        mm_xq(2, 0)
+        mm_xq(3, 0)
+        mm_xt(0, 1)
+        mm_xt(1, 1)
+
+        take_peak(0, 0)
+        cast(4)
+        cast(5)
+        take_sum(0, 0)
+        take_peak(1, 0)
+        quant(4)
+        quant(5)
+        take_sum(1, 0)
+        take_peak(2, 0)
+        cast(6)
+        cast(7)
+        take_peak(3, 0)
+        quant(6)
+        quant(7)
+        take_sum(2, 0)
+        take_sum(3, 0)
+
+        mm_xq(0, 1)
+        mm_xq(1, 1)
+        gt_ps = psum.tile([P, N], F32, name="gt_ps", tag="bank0")
+        nc.tensor.matmul_mx(out=gt_ps[:], lhsT=xg[:].bitcast(FP8X4), lhsT_scale=xgs[:],
+                            rhs=wg[:].bitcast(FP8X4), rhs_scale=wgs[:], start=True, stop=True)
+        mm_xt(2, 1)
+        mm_xt(3, 1)
+        mm_xq(2, 1)
+        mm_xq(3, 1)
+
+        gt = sb("gt", [P, N], F32)
+        nc.scalar.activation(out=gt[:].rearrange("p (r m) -> p r m", r=4), in_=gt_ps[:].rearrange("p (m r) -> p r m", r=4),
+                             func=ACT.Copy, scale=0.5)
+        g_ps = psum.tile([P, 4, B], F32, name="g_ps", tag="bank1")
+        for r in range(4):
+            nc.tensor.transpose(g_ps[:, r, :], gt[:, r * P:(r + 1) * P], ident[:])
+
+        def combine(r):
+            nc.vector.scalar_tensor_tensor(out=y[:, r, :], in0=peak[:, r, :], scalar=negmean[:, r:r + 1], in1=g_ps[:, r, :],
+                                           op0=ALU.add, op1=ALU.add)
+
+        take_peak(0, 1)
+        take_sum(1, 1)
+        take_peak(1, 1)
+        take_sum(0, 1)
+        take_peak(2, 1)
+        take_sum(3, 1)
+        take_peak(3, 1)
+        take_sum(2, 1)
+        combine(0)
+        combine(1)
+        out_rows = out_0.rearrange("(p r) b -> p r b", r=4)
+        nc.sync.dma_start(out=out_rows[:, 0:2, :], in_=y[:, 0:2, :])
+        combine(3)
+        combine(2)
+        nc.sync.dma_start(out=out_rows[:, 2:4, :], in_=y[:, 2:4, :])
+
+        y_bf = sb("y_bf", [P, 4 * B], BF16)
+        y_codes = sb("y_codes", [P, B], I32)
+        y_plane = sb("y_plane", [P, B], U8)
+        nc.vector.tensor_copy(out=y_bf[:].rearrange("p (c i r) -> p c r i", i=4, r=4),
+                              in_=y[:].rearrange("p r (c i) -> p c r i", i=4))
+        nc.vector.quantize_mx(out=y_codes[:].bitcast(FP8X4), scales=y_plane[:], in_=y_bf[:])
+        nc.sync.dma_start(out=out_1[0].rearrange("p c r -> p (c r)").bitcast(I32), in_=y_codes[:])
+        for q in range(4):
+            queue = nc.scalar if q % 2 == 0 else nc.sync
+            queue.dma_start(out=out_2[0, 4 * q:4 * q + 4, :].bitcast(I32), in_=y_plane[32 * q:32 * q + 4, :].bitcast(I32))

@@ -27,7 +27,6 @@ def tile_mix_peak_of_mixed_sum_pl_kernel(tc, xt_words, xt_scales, wa_words, wa_s
     nc = tc.nc
     with ExitStack() as ctx:
         keep = ctx.enter_context(tc.tile_pool(name="keep", bufs=1))
-        stage = ctx.enter_context(tc.tile_pool(name="stage", bufs=3))
         junk = ctx.enter_context(tc.tile_pool(name="junk", bufs=2))
         psum = ctx.enter_context(tc.psum_pool(name="psum", bufs=1))
         ctx.enter_context(tc.manual_schedule())
@@ -35,7 +34,7 @@ def tile_mix_peak_of_mixed_sum_pl_kernel(tc, xt_words, xt_scales, wa_words, wa_s
         def sb(name, shape, dtype):
             return keep.tile(shape, dtype, name=name, align_bytes=64)
 
-        def load_scales(queue, plane, scales, quads=range(4)):
+        def load_scales(queue, plane, scales, quads):
             for q in quads:
                 queue.dma_start(
                     out=plane[32 * q:32 * q + 4, :].bitcast(I32).rearrange("r (z c) -> r z c", z=scales.shape[0]),
@@ -51,42 +50,57 @@ def tile_mix_peak_of_mixed_sum_pl_kernel(tc, xt_words, xt_scales, wa_words, wa_s
         wgs = sb("wgs", [P, N], U8)
         xgs = sb("xgs", [P, B], U8)
         ident = sb("ident", [P, P], F32)
+        wa_raw = sb("wa_raw", [P, 2, N], I32)
+        wq_raw = sb("wq_raw", [P, 2 * N], U8)
+        wg = sb("wg", [P, N], I32)
+        xg = sb("xg", [P, B], I32)
+        xt = [sb("xt%d" % h, [P, 2, 2 * HALF], U8) for h in range(2)]
+        raw = [sb("raw%d" % c, [P, 4, QUARTER], F32) for c in range(4)]
 
-        nc.vector.memset(was_raw[:].bitcast(I32), 0)
-        nc.vector.memset(wqs_raw[:].bitcast(I32), 0)
-        nc.vector.memset(wgs[:].bitcast(I32), 0)
-        nc.vector.memset(xgs[:].bitcast(I32), 0)
+        for plane in (was_raw, xts, wqs_raw, wgs, xgs):
+            nc.vector.memset(plane[:].bitcast(I32), 0)
         warm = sb("warm", [P, 8], F32)
         warm2 = sb("warm2", [P, 8], F32)
-        nc.vector.memset(warm[:], 0.0)
+        nc.gpsimd.memset(warm[:], 0.0)
         nc.scalar.activation(out=warm2[:], in_=warm[:], func=ACT.Identity)
-        load_scales(nc.gpsimd, wqs_raw, wq_scales, (1,))
-        nc.gpsimd.memset(xts[:].bitcast(I32), 0)
-        load_scales(nc.gpsimd, wqs_raw, wq_scales, (2, 3))
+
         make_identity(nc, ident[:])
 
         def load_quarter(c):
-            raw = stage.tile([P, 4, QUARTER], F32, name="raw%d" % c, tag="stage", align_bytes=64)
-            nc.sync.dma_start(out=raw[:], in_=xq[:, c * QUARTER:(c + 1) * QUARTER].rearrange("(p j) t -> p j t", j=4))
-            return raw
+            nc.sync.dma_start(out=raw[c][:], in_=xq[:, c * QUARTER:(c + 1) * QUARTER].rearrange("(p j) t -> p j t", j=4))
 
         def load_xt(h):
-            words = sb("xt%d" % h, [P, 2, 2 * HALF], U8)
-            nc.sync.dma_start(out=words[:].bitcast(I32),
+            nc.sync.dma_start(out=xt[h][:].bitcast(I32),
                               in_=xt_words[:, :, 2 * h * HALF:2 * (h + 1) * HALF].rearrange("z p c -> p z c").bitcast(I32))
-            return words
 
-        wa_raw = stage.tile([P, 2, N], I32, name="wa_raw", tag="stage", align_bytes=64)
-        nc.sync.dma_start(out=wa_raw[:], in_=wa_words.rearrange("z p n t -> p z (n t)").bitcast(I32))
-        load_scales(nc.sync, was_raw, wa_scales)
-        xt = [load_xt(0)]
-        raw = [load_quarter(0), load_quarter(1)]
+        def load_wa():
+            nc.sync.dma_start(out=wa_raw[:], in_=wa_words.rearrange("z p n t -> p z (n t)").bitcast(I32))
 
-        wq_raw = sb("wq_raw", [P, 2 * N], U8)
-        load_scales(nc.scalar, xts, xt_scales)
-        nc.scalar.dma_start(out=wq_raw[:].bitcast(I32), in_=wq_words[0].bitcast(I32))
-        load_scales(nc.scalar, wqs_raw, wq_scales, (0,))
-        load_scales(nc.gpsimd, xgs, xg_scales)
+        def load_wq():
+            nc.sync.dma_start(out=wq_raw[:].bitcast(I32), in_=wq_words[0].bitcast(I32))
+
+        def load_wg():
+            nc.sync.dma_start(out=wg[:], in_=wg_words[0].rearrange("p n t -> p (n t)").bitcast(I32))
+
+        def load_xg():
+            nc.sync.dma_start(out=xg[:], in_=xg_words[0].rearrange("p n t -> p (n t)").bitcast(I32))
+
+        load_wa()
+        load_scales(nc.sync, was_raw, wa_scales, (0, 1, 2, 3,))
+        load_scales(nc.sync, xts, xt_scales, (0, 1,))
+        load_quarter(0)
+        load_scales(nc.sync, xts, xt_scales, (2, 3,))
+        load_xt(0)
+        load_wq()
+        load_quarter(1)
+        load_scales(nc.sync, wqs_raw, wq_scales, (0, 1, 2, 3,))
+        load_xt(1)
+        load_quarter(2)
+        load_quarter(3)
+        load_scales(nc.sync, wgs, wg_scales, (0, 1, 2, 3,))
+        load_wg()
+        load_xg()
+        load_scales(nc.gpsimd, xgs, xg_scales, (0, 1, 2, 3,))
 
         wa = [sb("wa%d" % z, [P, N], I32) for z in range(2)]
         was = sb("was", [P, 2 * N], U8)
@@ -97,22 +111,21 @@ def tile_mix_peak_of_mixed_sum_pl_kernel(tc, xt_words, xt_scales, wa_words, wa_s
             nc.vector.tensor_copy(out=wa[z][:].rearrange("p (r a i) -> p a r i", r=4, i=4),
                                   in_=wa_raw[:, z, :].rearrange("p (a i r) -> p a r i", r=4, i=4))
 
-        deal_wa(0)
-        deal_wa(1)
-        deal_scales(was, was_raw)
-
-        raw.append(load_quarter(2))
-        xt.append(load_xt(1))
+        def deal_wq():
+            nc.vector.tensor_copy(out=wq[:].rearrange("p (r a i e) -> p a r i e", r=4, i=8, e=2),
+                                  in_=wq_raw[:].rearrange("p (a i r e) -> p a r i e", r=4, i=8, e=2))
 
         codes = [sb("xq_codes%d" % h, [P, HALF], I32) for h in range(2)]
         planes = [sb("xq_plane%d" % h, [P, HALF], U8) for h in range(2)]
         rounded = [sb("xq_bf%d" % u, [P, 4 * UNIT], BF16) for u in range(T // UNIT)]
 
-        def cast(u):
+        def cast(u, engine):
             src = raw[u // 2][:, :, (u % 2) * UNIT:(u % 2 + 1) * UNIT].rearrange("p j (c i) -> p c j i", i=4)
             dst = rounded[u][:].rearrange("p (c i j) -> p c j i", i=4, j=4)
-            if u % 2 == 0:
+            if engine == "V":
                 nc.vector.tensor_copy(out=dst, in_=src)
+            elif engine == "G":
+                nc.gpsimd.tensor_scalar(out=dst, in0=src, scalar1=1.0, scalar2=0.0, op0=ALU.mult, op1=ALU.add)
             else:
                 nc.scalar.copy(out=dst, in_=src)
 
@@ -125,6 +138,10 @@ def tile_mix_peak_of_mixed_sum_pl_kernel(tc, xt_words, xt_scales, wa_words, wa_s
         for h in range(2):
             for r in range(4):
                 banks[r, h] = psum.tile([P, HALF], F32, name="z%d%d" % (r, h), tag="bank%d" % (4 * h + r))
+
+        def warm_pe():
+            nc.tensor.matmul_mx(out=banks[3, 1][:], lhsT=wa_raw[:, 0, 0:P].bitcast(FP8X4), lhsT_scale=was_raw[:, 0:P],
+                                rhs=wa_raw[:, 0, :].bitcast(FP8X4), rhs_scale=was_raw[:, 0:N], start=True, stop=True)
 
         def mm_xt(r, h):
             for z in range(2):
@@ -143,6 +160,11 @@ def tile_mix_peak_of_mixed_sum_pl_kernel(tc, xt_words, xt_scales, wa_words, wa_s
         part = sb("part", [P, 4], F32)
         negmean = sb("negmean", [P, 4], F32)
         y = sb("y", [P, 4, B], F32)
+        gt = sb("gt", [P, N], F32)
+        y_bf = sb("y_bf", [P, 4 * B], BF16)
+        y_codes = sb("y_codes", [P, B], I32)
+        y_plane = sb("y_plane", [P, B], U8)
+        late = {}
 
         def take_peak(r, h):
             nc.vector.tensor_reduce(out=peak[:, r, h * 64:(h + 1) * 64],
@@ -158,97 +180,102 @@ def tile_mix_peak_of_mixed_sum_pl_kernel(tc, xt_words, xt_scales, wa_words, wa_s
                 nc.scalar.activation(out=spill[:], in_=banks[r, h][:], func=ACT.Identity, scale=-1.0 / T,
                                      bias=part[:, r:r + 1], accum_out=negmean[:, r:r + 1])
 
-        for r in range(3):
-            mm_xt(r, 0)
+        def mm_g():
+            late["gt"] = psum.tile([P, N], F32, name="gt_ps", tag="bank0")
+            nc.tensor.matmul_mx(out=late["gt"][:], lhsT=xg[:].bitcast(FP8X4), lhsT_scale=xgs[:],
+                                rhs=wg[:].bitcast(FP8X4), rhs_scale=wgs[:], start=True, stop=True)
 
-        cast(0)
-        cast(1)
-        nc.vector.tensor_copy(out=wq[:].rearrange("p (r a i e) -> p a r i e", r=4, i=8, e=2),
-                              in_=wq_raw[:].rearrange("p (a i r e) -> p a r i e", r=4, i=8, e=2))
+        def copy_g():
+            nc.scalar.activation(out=gt[:].rearrange("p (r m) -> p r m", r=4),
+                                 in_=late["gt"][:].rearrange("p (m r) -> p r m", r=4), func=ACT.Copy, scale=0.5)
+
+        def turn_g():
+            late["g"] = psum.tile([P, 4, B], F32, name="g_ps", tag="bank1")
+            for r in range(4):
+                nc.tensor.transpose(late["g"][:, r, :], gt[:, r * P:(r + 1) * P], ident[:])
+
+        def combine(r, lo, hi):
+            nc.vector.scalar_tensor_tensor(out=y[:, r, lo:hi], in0=peak[:, r, lo:hi], scalar=negmean[:, r:r + 1],
+                                           in1=late["g"][:, r, lo:hi], op0=ALU.add, op1=ALU.add)
+
+        out_rows = out_0.rearrange("(p r) b -> p r b", r=4)
+
+        def store_y(a, b):
+            nc.sync.dma_start(out=out_rows[:, a:b, :], in_=y[:, a:b, :])
+
+        def round_y(lo, hi):
+            nc.vector.tensor_copy(out=y_bf[:, 4 * lo:4 * hi].rearrange("p (c i r) -> p c r i", i=4, r=4),
+                                  in_=y[:, :, lo:hi].rearrange("p r (c i) -> p c r i", i=4))
+
+        def quant_y(lo, hi):
+            nc.vector.quantize_mx(out=y_codes[:, lo:hi].bitcast(FP8X4), scales=y_plane[:, lo:hi], in_=y_bf[:, 4 * lo:4 * hi])
+
+        for w in range(4):
+            warm_pe()
+        deal_wa(0)
+        deal_wa(1)
+        deal_scales(was, was_raw)
+        cast(0, "V")
+        cast(1, "S")
+        for r in range(4):
+            mm_xt(r, 0)
         quant(0)
         quant(1)
-
-        raw.append(load_quarter(3))
-        wg = sb("wg", [P, N], I32)
-        xg = sb("xg", [P, B], I32)
-        nc.sync.dma_start(out=wg[:], in_=wg_words[0].rearrange("p n t -> p (n t)").bitcast(I32))
-        nc.sync.dma_start(out=xg[:], in_=xg_words[0].rearrange("p n t -> p (n t)").bitcast(I32))
-        load_scales(nc.sync, wgs, wg_scales)
-
-        cast(2)
-        cast(3)
+        deal_wq()
+        cast(2, "V")
+        cast(3, "S")
         deal_scales(wqs, wqs_raw)
         quant(2)
         quant(3)
-
-        mm_xq(0, 0)
-        mm_xq(1, 0)
-        mm_xt(3, 0)
-        mm_xq(2, 0)
-        mm_xq(3, 0)
-        mm_xt(0, 1)
-        mm_xt(1, 1)
-
+        for r in range(4):
+            mm_xq(r, 0)
+        cast(4, "V")
+        cast(5, "S")
         take_peak(0, 0)
-        cast(4)
-        cast(5)
-        take_sum(0, 0)
-        take_peak(1, 0)
+        take_sum(1, 0)
         quant(4)
         quant(5)
-        take_sum(1, 0)
-        take_peak(2, 0)
-        cast(6)
-        cast(7)
-        take_peak(3, 0)
+        cast(6, "V")
+        cast(7, "V")
         quant(6)
         quant(7)
+        take_sum(0, 0)
+        take_peak(1, 0)
         take_sum(2, 0)
         take_sum(3, 0)
-
-        mm_xq(0, 1)
-        mm_xq(1, 1)
-        gt_ps = psum.tile([P, N], F32, name="gt_ps", tag="bank0")
-        nc.tensor.matmul_mx(out=gt_ps[:], lhsT=xg[:].bitcast(FP8X4), lhsT_scale=xgs[:],
-                            rhs=wg[:].bitcast(FP8X4), rhs_scale=wgs[:], start=True, stop=True)
+        take_peak(2, 0)
+        take_peak(3, 0)
+        mm_xt(0, 1)
+        mm_xt(1, 1)
         mm_xt(2, 1)
-        mm_xt(3, 1)
+        mm_xq(0, 1)
+        mm_g()
+        mm_xq(1, 1)
         mm_xq(2, 1)
+        mm_xt(3, 1)
         mm_xq(3, 1)
-
-        gt = sb("gt", [P, N], F32)
-        nc.scalar.activation(out=gt[:].rearrange("p (r m) -> p r m", r=4), in_=gt_ps[:].rearrange("p (m r) -> p r m", r=4),
-                             func=ACT.Copy, scale=0.5)
-        g_ps = psum.tile([P, 4, B], F32, name="g_ps", tag="bank1")
-        for r in range(4):
-            nc.tensor.transpose(g_ps[:, r, :], gt[:, r * P:(r + 1) * P], ident[:])
-
-        def combine(r):
-            nc.vector.scalar_tensor_tensor(out=y[:, r, :], in0=peak[:, r, :], scalar=negmean[:, r:r + 1], in1=g_ps[:, r, :],
-                                           op0=ALU.add, op1=ALU.add)
-
-        take_peak(0, 1)
-        take_sum(1, 1)
-        take_peak(1, 1)
         take_sum(0, 1)
-        take_peak(2, 1)
-        take_sum(3, 1)
-        take_peak(3, 1)
+        copy_g()
+        turn_g()
+        take_peak(0, 1)
+        take_peak(1, 1)
         take_sum(2, 1)
-        combine(0)
-        combine(1)
-        out_rows = out_0.rearrange("(p r) b -> p r b", r=4)
-        nc.sync.dma_start(out=out_rows[:, 0:2, :], in_=y[:, 0:2, :])
-        combine(3)
-        combine(2)
-        nc.sync.dma_start(out=out_rows[:, 2:4, :], in_=y[:, 2:4, :])
+        take_sum(3, 1)
+        take_sum(1, 1)
+        take_peak(2, 1)
+        combine(0, 0, 128)
+        combine(2, 0, 128)
+        combine(3, 0, 64)
+        take_peak(3, 1)
+        combine(1, 0, 128)
+        store_y(0, 2)
+        combine(3, 64, 128)
+        store_y(2, 4)
+        round_y(0, 64)
+        round_y(64, 128)
+        quant_y(0, 64)
+        quant_y(64, 128)
 
-        y_bf = sb("y_bf", [P, 4 * B], BF16)
-        y_codes = sb("y_codes", [P, B], I32)
-        y_plane = sb("y_plane", [P, B], U8)
-        nc.vector.tensor_copy(out=y_bf[:].rearrange("p (c i r) -> p c r i", i=4, r=4),
-                              in_=y[:].rearrange("p r (c i) -> p c r i", i=4))
-        nc.vector.quantize_mx(out=y_codes[:].bitcast(FP8X4), scales=y_plane[:], in_=y_bf[:])
         nc.sync.dma_start(out=out_1[0].rearrange("p c r -> p (c r)").bitcast(I32), in_=y_codes[:])
         for q in range(4):
             queue = nc.scalar if q % 2 == 0 else nc.sync

@@ -16,10 +16,15 @@ ALU = mybir.AluOpType
 ACT = mybir.ActivationFunctionType
 
 P = 128
+PACK = 4
+QUADRANT = 32
+K_PASSES = K // (P * PACK)
 HALF = 512
 QUARTER = 256
 UNIT = 128
 GROUP = 8
+B_HALF = HALF // GROUP
+WARM_PASSES = 4
 
 
 def tile_mix_peak_of_mixed_sum_pl_kernel(tc, xt_words, xt_scales, wa_words, wa_scales, xq, wq_words, wq_scales,
@@ -27,256 +32,226 @@ def tile_mix_peak_of_mixed_sum_pl_kernel(tc, xt_words, xt_scales, wa_words, wa_s
     nc = tc.nc
     with ExitStack() as ctx:
         keep = ctx.enter_context(tc.tile_pool(name="keep", bufs=1))
-        junk = ctx.enter_context(tc.tile_pool(name="junk", bufs=2))
+        spare = ctx.enter_context(tc.tile_pool(name="spare", bufs=2))
         psum = ctx.enter_context(tc.psum_pool(name="psum", bufs=1))
         ctx.enter_context(tc.manual_schedule())
 
-        def sb(name, shape, dtype):
+        def sbuf(name, shape, dtype):
             return keep.tile(shape, dtype, name=name, align_bytes=64)
 
-        def load_scales(queue, plane, scales, quads):
-            for q in quads:
-                queue.dma_start(
-                    out=plane[32 * q:32 * q + 4, :].bitcast(I32).rearrange("r (z c) -> r z c", z=scales.shape[0]),
-                    in_=scales[:, 4 * q:4 * q + 4, :].rearrange("z r c -> r z c").bitcast(I32))
+        wa_raw = sbuf("wa_raw", [P, K_PASSES, N], I32)
+        wq_raw = sbuf("wq_raw", [P, 2 * N], U8)
+        wg = sbuf("wg", [P, N], I32)
+        xg = sbuf("xg", [P, B], I32)
+        xt = [sbuf("xt%d" % h, [P, K_PASSES, 2 * HALF], U8) for h in range(T // HALF)]
+        xq_raw = [sbuf("xq_raw%d" % c, [P, PACK, QUARTER], F32) for c in range(T // QUARTER)]
+        wa_plane_raw = sbuf("wa_plane_raw", [P, K_PASSES * N], U8)
+        wq_plane_raw = sbuf("wq_plane_raw", [P, N], U8)
+        xt_plane = sbuf("xt_plane", [P, K_PASSES * T], U8)
+        wg_plane = sbuf("wg_plane", [P, N], U8)
+        xg_plane = sbuf("xg_plane", [P, B], U8)
+        identity = sbuf("identity", [P, P], F32)
 
-        def deal_scales(dst, raw):
-            nc.vector.tensor_copy(out=dst[:].rearrange("p (z r a i) -> p z a r i", r=4, a=8, i=16),
-                                  in_=raw[:].rearrange("p (z a i r) -> p z a r i", r=4, a=8, i=16))
-
-        was_raw = sb("was_raw", [P, 2 * N], U8)
-        wqs_raw = sb("wqs_raw", [P, N], U8)
-        xts = sb("xts", [P, 2 * T], U8)
-        wgs = sb("wgs", [P, N], U8)
-        xgs = sb("xgs", [P, B], U8)
-        ident = sb("ident", [P, P], F32)
-        wa_raw = sb("wa_raw", [P, 2, N], I32)
-        wq_raw = sb("wq_raw", [P, 2 * N], U8)
-        wg = sb("wg", [P, N], I32)
-        xg = sb("xg", [P, B], I32)
-        xt = [sb("xt%d" % h, [P, 2, 2 * HALF], U8) for h in range(2)]
-        raw = [sb("raw%d" % c, [P, 4, QUARTER], F32) for c in range(4)]
-
-        for plane in (was_raw, xts, wqs_raw, wgs, xgs):
+        for plane in (wa_plane_raw, xt_plane, wq_plane_raw, wg_plane, xg_plane):
             nc.vector.memset(plane[:].bitcast(I32), 0)
-        warm = sb("warm", [P, 8], F32)
-        warm2 = sb("warm2", [P, 8], F32)
-        nc.gpsimd.memset(warm[:], 0.0)
-        nc.scalar.activation(out=warm2[:], in_=warm[:], func=ACT.Identity)
+        make_identity(nc, identity[:])
 
-        make_identity(nc, ident[:])
+        def load_scale_rows(queue, plane, scales, rows):
+            by_row = scales.rearrange("z (q s) c -> s q z c", s=PACK)
+            for s in rows:
+                queue.dma_start(out=plane[s:P:QUADRANT, :].bitcast(I32).rearrange("q (z c) -> q z c", z=scales.shape[0]),
+                                in_=by_row[s].bitcast(I32))
 
-        def load_quarter(c):
-            nc.sync.dma_start(out=raw[c][:], in_=xq[:, c * QUARTER:(c + 1) * QUARTER].rearrange("(p j) t -> p j t", j=4))
+        def load_xq(c):
+            tokens = xq[:, c * QUARTER:(c + 1) * QUARTER]
+            nc.sync.dma_start(out=xq_raw[c][:], in_=tokens.rearrange("(p j) t -> p j t", j=PACK))
 
         def load_xt(h):
-            nc.sync.dma_start(out=xt[h][:].bitcast(I32),
-                              in_=xt_words[:, :, 2 * h * HALF:2 * (h + 1) * HALF].rearrange("z p c -> p z c").bitcast(I32))
+            words = xt_words[:, :, 2 * h * HALF:2 * (h + 1) * HALF]
+            nc.sync.dma_start(out=xt[h][:].bitcast(I32), in_=words.rearrange("z p c -> p z c").bitcast(I32))
 
-        def load_wa():
-            nc.sync.dma_start(out=wa_raw[:], in_=wa_words.rearrange("z p n t -> p z (n t)").bitcast(I32))
-
-        def load_wq():
-            nc.sync.dma_start(out=wq_raw[:].bitcast(I32), in_=wq_words[0].bitcast(I32))
-
-        def load_wg():
-            nc.sync.dma_start(out=wg[:], in_=wg_words[0].rearrange("p n t -> p (n t)").bitcast(I32))
-
-        def load_xg():
-            nc.sync.dma_start(out=xg[:], in_=xg_words[0].rearrange("p n t -> p (n t)").bitcast(I32))
-
-        load_wa()
-        load_scales(nc.sync, was_raw, wa_scales, (0, 1, 2, 3,))
-        load_scales(nc.sync, xts, xt_scales, (0, 1,))
-        load_quarter(0)
-        load_scales(nc.sync, xts, xt_scales, (2, 3,))
+        all_rows = range(PACK)
+        nc.sync.dma_start(out=wa_raw[:], in_=wa_words.rearrange("z p n j -> p z (n j)").bitcast(I32))
+        load_scale_rows(nc.sync, wa_plane_raw, wa_scales, all_rows)
+        load_scale_rows(nc.sync, xt_plane, xt_scales, all_rows[:2])
+        load_xq(0)
+        load_scale_rows(nc.sync, xt_plane, xt_scales, all_rows[2:])
         load_xt(0)
-        load_wq()
-        load_quarter(1)
-        load_scales(nc.sync, wqs_raw, wq_scales, (0, 1, 2, 3,))
+        nc.sync.dma_start(out=wq_raw[:].bitcast(I32), in_=wq_words[0].bitcast(I32))
+        load_xq(1)
+        load_scale_rows(nc.sync, wq_plane_raw, wq_scales, all_rows)
+        load_xq(2)
         load_xt(1)
-        load_quarter(2)
-        load_quarter(3)
-        load_scales(nc.sync, wgs, wg_scales, (0, 1, 2, 3,))
-        load_wg()
-        load_xg()
-        load_scales(nc.gpsimd, xgs, xg_scales, (0, 1, 2, 3,))
+        load_xq(3)
+        load_scale_rows(nc.sync, wg_plane, wg_scales, all_rows)
+        nc.sync.dma_start(out=wg[:], in_=wg_words[0].rearrange("p n j -> p (n j)").bitcast(I32))
+        nc.sync.dma_start(out=xg[:], in_=xg_words[0].rearrange("p b j -> p (b j)").bitcast(I32))
+        load_scale_rows(nc.gpsimd, xg_plane, xg_scales, all_rows)
 
-        wa = [sb("wa%d" % z, [P, N], I32) for z in range(2)]
-        was = sb("was", [P, 2 * N], U8)
-        wq = sb("wq", [P, 2 * N], U8)
-        wqs = sb("wqs", [P, N], U8)
+        wa = [sbuf("wa%d" % z, [P, N], I32) for z in range(K_PASSES)]
+        wq = sbuf("wq", [P, 2 * N], U8)
+        wa_plane = sbuf("wa_plane", [P, K_PASSES * N], U8)
+        wq_plane = sbuf("wq_plane", [P, N], U8)
 
         def deal_wa(z):
-            nc.vector.tensor_copy(out=wa[z][:].rearrange("p (r a i) -> p a r i", r=4, i=4),
-                                  in_=wa_raw[:, z, :].rearrange("p (a i r) -> p a r i", r=4, i=4))
+            nc.vector.tensor_copy(out=wa[z][:].rearrange("p (r a i) -> p a r i", r=PACK, i=4),
+                                  in_=wa_raw[:, z, :].rearrange("p (a i r) -> p a r i", r=PACK, i=4))
 
         def deal_wq():
-            nc.vector.tensor_copy(out=wq[:].rearrange("p (r a i e) -> p a r i e", r=4, i=8, e=2),
-                                  in_=wq_raw[:].rearrange("p (a i r e) -> p a r i e", r=4, i=8, e=2))
+            nc.vector.tensor_copy(out=wq[:].rearrange("p (r a i e) -> p a r i e", r=PACK, i=8, e=2),
+                                  in_=wq_raw[:].rearrange("p (a i r e) -> p a r i e", r=PACK, i=8, e=2))
 
-        codes = [sb("xq_codes%d" % h, [P, HALF], I32) for h in range(2)]
-        planes = [sb("xq_plane%d" % h, [P, HALF], U8) for h in range(2)]
-        rounded = [sb("xq_bf%d" % u, [P, 4 * UNIT], BF16) for u in range(T // UNIT)]
+        def deal_plane(dealt, raw):
+            nc.vector.tensor_copy(out=dealt[:].rearrange("p (z r a i) -> p z a r i", r=PACK, a=P // 16, i=16),
+                                  in_=raw[:].rearrange("p (z a i r) -> p z a r i", r=PACK, a=P // 16, i=16))
 
-        def cast(u, engine):
-            src = raw[u // 2][:, :, (u % 2) * UNIT:(u % 2 + 1) * UNIT].rearrange("p j (c i) -> p c j i", i=4)
-            dst = rounded[u][:].rearrange("p (c i j) -> p c j i", i=4, j=4)
-            if engine == "V":
-                nc.vector.tensor_copy(out=dst, in_=src)
-            elif engine == "G":
-                nc.gpsimd.tensor_scalar(out=dst, in0=src, scalar1=1.0, scalar2=0.0, op0=ALU.mult, op1=ALU.add)
-            else:
-                nc.scalar.copy(out=dst, in_=src)
+        xq_bf = [sbuf("xq_bf%d" % u, [P, PACK * UNIT], BF16) for u in range(T // UNIT)]
+        xq_codes = [sbuf("xq_codes%d" % h, [P, HALF], I32) for h in range(T // HALF)]
+        xq_plane = [sbuf("xq_plane%d" % h, [P, HALF], U8) for h in range(T // HALF)]
 
-        def quant(u):
-            h, c = divmod(u, 4)
-            cols = slice(c * UNIT, (c + 1) * UNIT)
-            nc.vector.quantize_mx(out=codes[h][:, cols].bitcast(FP8X4), scales=planes[h][:, cols], in_=rounded[u][:])
+        def rounding_views(u):
+            c, first = divmod(u * UNIT, QUARTER)
+            return (xq_bf[u][:].rearrange("p (a i j) -> p a j i", i=4, j=PACK),
+                    xq_raw[c][:, :, first:first + UNIT].rearrange("p j (a i) -> p a j i", i=4))
 
-        banks = {}
-        for h in range(2):
-            for r in range(4):
-                banks[r, h] = psum.tile([P, HALF], F32, name="z%d%d" % (r, h), tag="bank%d" % (4 * h + r))
+        def round_on_vector(u):
+            rounded, raw = rounding_views(u)
+            nc.vector.tensor_copy(out=rounded, in_=raw)
 
-        def warm_pe():
-            nc.tensor.matmul_mx(out=banks[3, 1][:], lhsT=wa_raw[:, 0, 0:P].bitcast(FP8X4), lhsT_scale=was_raw[:, 0:P],
-                                rhs=wa_raw[:, 0, :].bitcast(FP8X4), rhs_scale=was_raw[:, 0:N], start=True, stop=True)
+        def round_on_scalar(u):
+            rounded, raw = rounding_views(u)
+            nc.scalar.activation(out=rounded, in_=raw, func=ACT.Copy)
 
-        def mm_xt(r, h):
-            for z in range(2):
-                nc.tensor.matmul_mx(out=banks[r, h][:], lhsT=wa[z][:, r * P:(r + 1) * P].bitcast(FP8X4),
-                                    lhsT_scale=was[:, z * N + r * P:z * N + (r + 1) * P],
+        def quantise_xq(u):
+            h, first = divmod(u * UNIT, HALF)
+            cols = slice(first, first + UNIT)
+            nc.vector.quantize_mx(out=xq_codes[h][:, cols].bitcast(FP8X4), scales=xq_plane[h][:, cols], in_=xq_bf[u][:])
+
+        z_bank = {}
+        for h in range(T // HALF):
+            for r in range(PACK):
+                z_bank[r, h] = psum.tile([P, HALF], F32, name="z%d%d" % (r, h), tag="bank%d" % (PACK * h + r))
+
+        def xt_passes(r, h):
+            for z in range(K_PASSES):
+                nc.tensor.matmul_mx(out=z_bank[r, h][:], lhsT=wa[z][:, r * P:(r + 1) * P].bitcast(FP8X4),
+                                    lhsT_scale=wa_plane[:, z * N + r * P:z * N + (r + 1) * P],
                                     rhs=xt[h][:, z, :].bitcast(FP4X4),
-                                    rhs_scale=xts[:, z * T + h * HALF:z * T + (h + 1) * HALF],
+                                    rhs_scale=xt_plane[:, z * T + h * HALF:z * T + (h + 1) * HALF],
                                     start=(z == 0), stop=False)
 
-        def mm_xq(r, h):
-            nc.tensor.matmul_mx(out=banks[r, h][:], lhsT=wq[:, 2 * r * P:2 * (r + 1) * P].bitcast(FP4X4),
-                                lhsT_scale=wqs[:, r * P:(r + 1) * P],
-                                rhs=codes[h][:].bitcast(FP8X4), rhs_scale=planes[h][:], start=False, stop=True)
+        def xq_pass(r, h):
+            nc.tensor.matmul_mx(out=z_bank[r, h][:], lhsT=wq[:, 2 * r * P:2 * (r + 1) * P].bitcast(FP4X4),
+                                lhsT_scale=wq_plane[:, r * P:(r + 1) * P],
+                                rhs=xq_codes[h][:].bitcast(FP8X4), rhs_scale=xq_plane[h][:], start=False, stop=True)
 
-        peak = sb("peak", [P, 4, B], F32)
-        part = sb("part", [P, 4], F32)
-        negmean = sb("negmean", [P, 4], F32)
-        y = sb("y", [P, 4, B], F32)
-        gt = sb("gt", [P, N], F32)
-        y_bf = sb("y_bf", [P, 4 * B], BF16)
-        y_codes = sb("y_codes", [P, B], I32)
-        y_plane = sb("y_plane", [P, B], U8)
-        late = {}
+        peak = sbuf("peak", [P, PACK, B], F32)
+        first_share = sbuf("first_share", [P, PACK], F32)
+        minus_mean = sbuf("minus_mean", [P, PACK], F32)
 
-        def take_peak(r, h):
-            nc.vector.tensor_reduce(out=peak[:, r, h * 64:(h + 1) * 64],
-                                    in_=banks[r, h][:].rearrange("p (b j) -> p b j", j=GROUP),
+        def take_peaks(r, h):
+            nc.vector.tensor_reduce(out=peak[:, r, h * B_HALF:(h + 1) * B_HALF],
+                                    in_=z_bank[r, h][:].rearrange("p (b i) -> p b i", i=GROUP),
                                     axis=mybir.AxisListType.X, op=ALU.max)
 
         def take_sum(r, h):
-            spill = junk.tile([P, HALF], BF16, name="spill")
+            unread = spare.tile([P, HALF], BF16, name="unread")
             if h == 0:
-                nc.scalar.activation(out=spill[:], in_=banks[r, h][:], func=ACT.Identity, scale=-1.0 / (T * HALF),
-                                     accum_out=part[:, r:r + 1])
+                nc.scalar.activation(out=unread[:], in_=z_bank[r, h][:], func=ACT.Identity, scale=-1.0 / (T * HALF),
+                                     accum_out=first_share[:, r:r + 1])
             else:
-                nc.scalar.activation(out=spill[:], in_=banks[r, h][:], func=ACT.Identity, scale=-1.0 / T,
-                                     bias=part[:, r:r + 1], accum_out=negmean[:, r:r + 1])
+                nc.scalar.activation(out=unread[:], in_=z_bank[r, h][:], func=ACT.Identity, scale=-1.0 / T,
+                                     bias=first_share[:, r:r + 1], accum_out=minus_mean[:, r:r + 1])
 
-        def mm_g():
-            late["gt"] = psum.tile([P, N], F32, name="gt_ps", tag="bank0")
-            nc.tensor.matmul_mx(out=late["gt"][:], lhsT=xg[:].bitcast(FP8X4), lhsT_scale=xgs[:],
-                                rhs=wg[:].bitcast(FP8X4), rhs_scale=wgs[:], start=True, stop=True)
+        for warm_pass in range(WARM_PASSES):
+            nc.tensor.matmul_mx(out=z_bank[PACK - 1, 1][:], lhsT=wa_raw[:, 0, 0:P].bitcast(FP8X4),
+                                lhsT_scale=wa_plane_raw[:, 0:P], rhs=wa_raw[:, 0, :].bitcast(FP8X4),
+                                rhs_scale=wa_plane_raw[:, 0:N], start=True, stop=True)
 
-        def copy_g():
-            nc.scalar.activation(out=gt[:].rearrange("p (r m) -> p r m", r=4),
-                                 in_=late["gt"][:].rearrange("p (m r) -> p r m", r=4), func=ACT.Copy, scale=0.5)
-
-        def turn_g():
-            late["g"] = psum.tile([P, 4, B], F32, name="g_ps", tag="bank1")
-            for r in range(4):
-                nc.tensor.transpose(late["g"][:, r, :], gt[:, r * P:(r + 1) * P], ident[:])
-
-        def combine(r, lo, hi):
-            nc.vector.scalar_tensor_tensor(out=y[:, r, lo:hi], in0=peak[:, r, lo:hi], scalar=negmean[:, r:r + 1],
-                                           in1=late["g"][:, r, lo:hi], op0=ALU.add, op1=ALU.add)
-
-        out_rows = out_0.rearrange("(p r) b -> p r b", r=4)
-
-        def store_y(a, b):
-            nc.sync.dma_start(out=out_rows[:, a:b, :], in_=y[:, a:b, :])
-
-        def round_y(lo, hi):
-            nc.vector.tensor_copy(out=y_bf[:, 4 * lo:4 * hi].rearrange("p (c i r) -> p c r i", i=4, r=4),
-                                  in_=y[:, :, lo:hi].rearrange("p r (c i) -> p c r i", i=4))
-
-        def quant_y(lo, hi):
-            nc.vector.quantize_mx(out=y_codes[:, lo:hi].bitcast(FP8X4), scales=y_plane[:, lo:hi], in_=y_bf[:, 4 * lo:4 * hi])
-
-        for w in range(4):
-            warm_pe()
-        deal_wa(0)
-        deal_wa(1)
-        deal_scales(was, was_raw)
-        cast(0, "V")
-        cast(1, "S")
-        for r in range(4):
-            mm_xt(r, 0)
-        quant(0)
-        quant(1)
+        for z in range(K_PASSES):
+            deal_wa(z)
+        deal_plane(wa_plane, wa_plane_raw)
+        round_on_vector(0)
+        round_on_scalar(1)
+        quantise_xq(0)
+        quantise_xq(1)
         deal_wq()
-        cast(2, "V")
-        cast(3, "S")
-        deal_scales(wqs, wqs_raw)
-        quant(2)
-        quant(3)
-        for r in range(4):
-            mm_xq(r, 0)
-        cast(4, "V")
-        cast(5, "S")
-        take_peak(0, 0)
-        take_sum(1, 0)
-        quant(4)
-        quant(5)
-        cast(6, "V")
-        cast(7, "V")
-        quant(6)
-        quant(7)
-        take_sum(0, 0)
-        take_peak(1, 0)
-        take_sum(2, 0)
-        take_sum(3, 0)
-        take_peak(2, 0)
-        take_peak(3, 0)
-        mm_xt(0, 1)
-        mm_xt(1, 1)
-        mm_xt(2, 1)
-        mm_xq(0, 1)
-        mm_g()
-        mm_xq(1, 1)
-        mm_xq(2, 1)
-        mm_xt(3, 1)
-        mm_xq(3, 1)
-        take_sum(0, 1)
-        copy_g()
-        turn_g()
-        take_peak(0, 1)
-        take_peak(1, 1)
-        take_sum(2, 1)
-        take_sum(3, 1)
-        take_sum(1, 1)
-        take_peak(2, 1)
-        combine(0, 0, 128)
-        combine(2, 0, 128)
-        combine(3, 0, 64)
-        take_peak(3, 1)
-        combine(1, 0, 128)
-        store_y(0, 2)
-        combine(3, 64, 128)
-        store_y(2, 4)
-        round_y(0, 64)
-        round_y(64, 128)
-        quant_y(0, 64)
-        quant_y(64, 128)
+        round_on_vector(2)
+        round_on_scalar(3)
+        deal_plane(wq_plane, wq_plane_raw)
+        quantise_xq(2)
+        quantise_xq(3)
+        for r in range(PACK):
+            xt_passes(r, 0)
+        for r in range(PACK):
+            xq_pass(r, 0)
 
-        nc.sync.dma_start(out=out_1[0].rearrange("p c r -> p (c r)").bitcast(I32), in_=y_codes[:])
-        for q in range(4):
-            queue = nc.scalar if q % 2 == 0 else nc.sync
-            queue.dma_start(out=out_2[0, 4 * q:4 * q + 4, :].bitcast(I32), in_=y_plane[32 * q:32 * q + 4, :].bitcast(I32))
+        round_on_vector(4)
+        round_on_scalar(5)
+        take_peaks(0, 0)
+        quantise_xq(4)
+        quantise_xq(5)
+        take_sum(1, 0)
+        take_sum(0, 0)
+        take_peaks(2, 0)
+        round_on_vector(6)
+        round_on_vector(7)
+        quantise_xq(6)
+        quantise_xq(7)
+        take_sum(3, 0)
+        take_sum(2, 0)
+        take_peaks(1, 0)
+        take_peaks(3, 0)
+
+        for r in range(PACK):
+            xt_passes(r, 1)
+        g_turned = psum.tile([P, N], F32, name="g_turned", tag="bank0")
+        nc.tensor.matmul_mx(out=g_turned[:], lhsT=xg[:].bitcast(FP8X4), lhsT_scale=xg_plane[:],
+                            rhs=wg[:].bitcast(FP8X4), rhs_scale=wg_plane[:], start=True, stop=True)
+        for r in range(PACK):
+            xq_pass(r, 1)
+        half_g_turned = sbuf("half_g_turned", [P, N], F32)
+        nc.scalar.activation(out=half_g_turned[:].rearrange("b (r p) -> b r p", r=PACK),
+                             in_=g_turned[:].rearrange("b (p r) -> b r p", r=PACK), func=ACT.Copy, scale=0.5)
+        half_g = psum.tile([P, PACK, B], F32, name="half_g", tag="bank1")
+        for r in range(PACK):
+            nc.tensor.transpose(half_g[:, r, :], half_g_turned[:, r * P:(r + 1) * P], identity[:])
+
+        y = sbuf("y", [P, PACK, B], F32)
+        out_rows = out_0.rearrange("(p r) b -> p r b", r=PACK)
+        low, high, every = slice(0, B_HALF), slice(B_HALF, B), slice(0, B)
+
+        def combine(r, groups):
+            nc.vector.scalar_tensor_tensor(out=y[:, r, groups], in0=peak[:, r, groups], scalar=minus_mean[:, r:r + 1],
+                                           in1=half_g[:, r, groups], op0=ALU.add, op1=ALU.add)
+
+        take_peaks(0, 1)
+        take_sum(1, 1)
+        take_peaks(2, 1)
+        take_sum(0, 1)
+        take_peaks(1, 1)
+        take_sum(3, 1)
+        combine(0, every)
+        combine(1, every)
+        nc.sync.dma_start(out=out_rows[:, 0:2, :], in_=y[:, 0:2, :])
+        combine(3, low)
+        take_peaks(3, 1)
+        take_sum(2, 1)
+        combine(2, every)
+        combine(3, high)
+        nc.sync.dma_start(out=out_rows[:, 2:PACK, :], in_=y[:, 2:PACK, :])
+
+        y_bf = sbuf("y_bf", [P, B, PACK], BF16)
+        y_codes = sbuf("y_codes", [P, B], I32)
+        y_plane = sbuf("y_plane", [P, B], U8)
+        for groups in (low, high):
+            nc.vector.tensor_copy(out=y_bf[:, groups, :].rearrange("p (a i) r -> p a r i", i=4),
+                                  in_=y[:, :, groups].rearrange("p r (a i) -> p a r i", i=4))
+        for groups in (low, high):
+            nc.vector.quantize_mx(out=y_codes[:, groups].bitcast(FP8X4), scales=y_plane[:, groups],
+                                  in_=y_bf[:, groups, :].rearrange("p b r -> p (b r)"))
+
+        nc.sync.dma_start(out=out_1[0].rearrange("p b r -> p (b r)").bitcast(I32), in_=y_codes[:])
+        for q, queue in enumerate((nc.scalar, nc.sync, nc.scalar, nc.sync)):
+            queue.dma_start(out=out_2[0, PACK * q:PACK * (q + 1), :].bitcast(I32),
+                            in_=y_plane[QUADRANT * q:QUADRANT * q + PACK, :].bitcast(I32))

from contextlib import ExitStack

import concourse.mybir as mybir
from concourse.masks import make_identity

K, L, M, T, B, N = 1024, 512, 512, 1024, 128, 512
FLOPS = 2 * N * (K * T + L * T + M * B)

F32 = mybir.dt.float32
BF16 = mybir.dt.bfloat16
I32 = mybir.dt.int32
U8 = mybir.dt.uint8
FP8X4 = mybir.dt.float8_e4m3fn_x4
FP4X4 = mybir.dt.float4_e2m1fn_x4
ALU = mybir.AluOpType
ACT = mybir.ActivationFunctionType

P = 128
PACK = 4
QUADRANT = 32
K_PASSES = K // (P * PACK)
HALF = 512
QUARTER = 256
UNIT = 128
GROUP = 8
B_HALF = HALF // GROUP
WARM_PASSES = 4


def tile_mix_peak_of_mixed_sum_pl_kernel(tc, xt_words, xt_scales, wa_words, wa_scales, xq, wq_words, wq_scales,
                                              xg_words, xg_scales, wg_words, wg_scales, out_0, out_1, out_2):
    nc = tc.nc
    with ExitStack() as ctx:
        keep = ctx.enter_context(tc.tile_pool(name="keep", bufs=1))
        spare = ctx.enter_context(tc.tile_pool(name="spare", bufs=2))
        psum = ctx.enter_context(tc.psum_pool(name="psum", bufs=1))
        ctx.enter_context(tc.manual_schedule())

        def sbuf(name, shape, dtype):
            return keep.tile(shape, dtype, name=name, align_bytes=64)

        wa_raw = sbuf("wa_raw", [P, K_PASSES, N], I32)
        wq_raw = sbuf("wq_raw", [P, 2 * N], U8)
        wg = sbuf("wg", [P, N], I32)
        xg = sbuf("xg", [P, B], I32)
        xt = [sbuf("xt%d" % h, [P, K_PASSES, 2 * HALF], U8) for h in range(T // HALF)]
        xq_raw = [sbuf("xq_raw%d" % c, [P, PACK, QUARTER], F32) for c in range(T // QUARTER)]
        wa_plane_raw = sbuf("wa_plane_raw", [P, K_PASSES * N], U8)
        wq_plane_raw = sbuf("wq_plane_raw", [P, N], U8)
        xt_plane = sbuf("xt_plane", [P, K_PASSES * T], U8)
        wg_plane = sbuf("wg_plane", [P, N], U8)
        xg_plane = sbuf("xg_plane", [P, B], U8)
        identity = sbuf("identity", [P, P], F32)

        for plane in (wa_plane_raw, xt_plane, wq_plane_raw, wg_plane, xg_plane):
            nc.vector.memset(plane[:].bitcast(I32), 0)
        make_identity(nc, identity[:])

        def load_scale_rows(queue, plane, scales, rows):
            by_row = scales.rearrange("z (q s) c -> s q z c", s=PACK)
            for s in rows:
                queue.dma_start(out=plane[s:P:QUADRANT, :].bitcast(I32).rearrange("q (z c) -> q z c", z=scales.shape[0]),
                                in_=by_row[s].bitcast(I32))

        def load_xq(c):
            tokens = xq[:, c * QUARTER:(c + 1) * QUARTER]
            nc.sync.dma_start(out=xq_raw[c][:], in_=tokens.rearrange("(p j) t -> p j t", j=PACK))

        def load_xt(h):
            words = xt_words[:, :, 2 * h * HALF:2 * (h + 1) * HALF]
            nc.sync.dma_start(out=xt[h][:].bitcast(I32), in_=words.rearrange("z p c -> p z c").bitcast(I32))

        all_rows = range(PACK)
        nc.sync.dma_start(out=wa_raw[:], in_=wa_words.rearrange("z p n j -> p z (n j)").bitcast(I32))
        load_scale_rows(nc.sync, wa_plane_raw, wa_scales, all_rows)
        load_scale_rows(nc.sync, xt_plane, xt_scales, all_rows[:2])
        load_xq(0)
        load_scale_rows(nc.sync, xt_plane, xt_scales, all_rows[2:])
        load_xt(0)
        nc.sync.dma_start(out=wq_raw[:].bitcast(I32), in_=wq_words[0].bitcast(I32))
        load_xq(1)
        load_scale_rows(nc.sync, wq_plane_raw, wq_scales, all_rows)
        load_xq(2)
        load_xt(1)
        load_xq(3)
        load_scale_rows(nc.sync, wg_plane, wg_scales, all_rows)
        nc.sync.dma_start(out=wg[:], in_=wg_words[0].rearrange("p n j -> p (n j)").bitcast(I32))
        nc.sync.dma_start(out=xg[:], in_=xg_words[0].rearrange("p b j -> p (b j)").bitcast(I32))
        load_scale_rows(nc.gpsimd, xg_plane, xg_scales, all_rows)

        wa = [sbuf("wa%d" % z, [P, N], I32) for z in range(K_PASSES)]
        wq = sbuf("wq", [P, 2 * N], U8)
        wa_plane = sbuf("wa_plane", [P, K_PASSES * N], U8)
        wq_plane = sbuf("wq_plane", [P, N], U8)

        def deal_wa(z):
            nc.vector.tensor_copy(out=wa[z][:].rearrange("p (r a i) -> p a r i", r=PACK, i=4),
                                  in_=wa_raw[:, z, :].rearrange("p (a i r) -> p a r i", r=PACK, i=4))

        def deal_wq():
            nc.vector.tensor_copy(out=wq[:].rearrange("p (r a i e) -> p a r i e", r=PACK, i=8, e=2),
                                  in_=wq_raw[:].rearrange("p (a i r e) -> p a r i e", r=PACK, i=8, e=2))

        def deal_plane(dealt, raw):
            nc.vector.tensor_copy(out=dealt[:].rearrange("p (z r a i) -> p z a r i", r=PACK, a=P // 16, i=16),
                                  in_=raw[:].rearrange("p (z a i r) -> p z a r i", r=PACK, a=P // 16, i=16))

        xq_bf = [sbuf("xq_bf%d" % u, [P, PACK * UNIT], BF16) for u in range(T // UNIT)]
        xq_codes = [sbuf("xq_codes%d" % h, [P, HALF], I32) for h in range(T // HALF)]
        xq_plane = [sbuf("xq_plane%d" % h, [P, HALF], U8) for h in range(T // HALF)]

        def rounding_views(u):
            c, first = divmod(u * UNIT, QUARTER)
            return (xq_bf[u][:].rearrange("p (a i j) -> p a j i", i=4, j=PACK),
                    xq_raw[c][:, :, first:first + UNIT].rearrange("p j (a i) -> p a j i", i=4))

        def round_on_vector(u):
            rounded, raw = rounding_views(u)
            nc.vector.tensor_copy(out=rounded, in_=raw)

        def round_on_scalar(u):
            rounded, raw = rounding_views(u)
            nc.scalar.activation(out=rounded, in_=raw, func=ACT.Copy)

        def quantise_xq(u):
            h, first = divmod(u * UNIT, HALF)
            cols = slice(first, first + UNIT)
            nc.vector.quantize_mx(out=xq_codes[h][:, cols].bitcast(FP8X4), scales=xq_plane[h][:, cols], in_=xq_bf[u][:])

        z_bank = {}
        for h in range(T // HALF):
            for r in range(PACK):
                z_bank[r, h] = psum.tile([P, HALF], F32, name="z%d%d" % (r, h), tag="bank%d" % (PACK * h + r))

        def xt_passes(r, h):
            for z in range(K_PASSES):
                nc.tensor.matmul_mx(out=z_bank[r, h][:], lhsT=wa[z][:, r * P:(r + 1) * P].bitcast(FP8X4),
                                    lhsT_scale=wa_plane[:, z * N + r * P:z * N + (r + 1) * P],
                                    rhs=xt[h][:, z, :].bitcast(FP4X4),
                                    rhs_scale=xt_plane[:, z * T + h * HALF:z * T + (h + 1) * HALF],
                                    start=(z == 0), stop=False)

        def xq_pass(r, h):
            nc.tensor.matmul_mx(out=z_bank[r, h][:], lhsT=wq[:, 2 * r * P:2 * (r + 1) * P].bitcast(FP4X4),
                                lhsT_scale=wq_plane[:, r * P:(r + 1) * P],
                                rhs=xq_codes[h][:].bitcast(FP8X4), rhs_scale=xq_plane[h][:], start=False, stop=True)

        peak = sbuf("peak", [P, PACK, B], F32)
        first_share = sbuf("first_share", [P, PACK], F32)
        minus_mean = sbuf("minus_mean", [P, PACK], F32)

        def take_peaks(r, h):
            nc.vector.tensor_reduce(out=peak[:, r, h * B_HALF:(h + 1) * B_HALF],
                                    in_=z_bank[r, h][:].rearrange("p (b i) -> p b i", i=GROUP),
                                    axis=mybir.AxisListType.X, op=ALU.max)

        def take_sum(r, h):
            unread = spare.tile([P, HALF], BF16, name="unread")
            if h == 0:
                nc.scalar.activation(out=unread[:], in_=z_bank[r, h][:], func=ACT.Identity, scale=-1.0 / (T * HALF),
                                     accum_out=first_share[:, r:r + 1])
            else:
                nc.scalar.activation(out=unread[:], in_=z_bank[r, h][:], func=ACT.Identity, scale=-1.0 / T,
                                     bias=first_share[:, r:r + 1], accum_out=minus_mean[:, r:r + 1])

        for warm_pass in range(WARM_PASSES):
            nc.tensor.matmul_mx(out=z_bank[PACK - 1, 1][:], lhsT=wa_raw[:, 0, 0:P].bitcast(FP8X4),
                                lhsT_scale=wa_plane_raw[:, 0:P], rhs=wa_raw[:, 0, :].bitcast(FP8X4),
                                rhs_scale=wa_plane_raw[:, 0:N], start=True, stop=True)

        for z in range(K_PASSES):
            deal_wa(z)
        deal_plane(wa_plane, wa_plane_raw)
        round_on_vector(0)
        round_on_scalar(1)
        quantise_xq(0)
        quantise_xq(1)
        deal_wq()
        round_on_vector(2)
        round_on_scalar(3)
        deal_plane(wq_plane, wq_plane_raw)
        quantise_xq(2)
        quantise_xq(3)
        for r in range(PACK):
            xt_passes(r, 0)
        for r in range(PACK):
            xq_pass(r, 0)

        round_on_vector(4)
        round_on_scalar(5)
        take_peaks(0, 0)
        quantise_xq(4)
        quantise_xq(5)
        take_sum(1, 0)
        take_sum(0, 0)
        take_peaks(2, 0)
        round_on_vector(6)
        round_on_vector(7)
        quantise_xq(6)
        quantise_xq(7)
        take_sum(3, 0)
        take_sum(2, 0)
        take_peaks(1, 0)
        take_peaks(3, 0)

        for r in range(PACK):
            xt_passes(r, 1)
        g_turned = psum.tile([P, N], F32, name="g_turned", tag="bank0")
        nc.tensor.matmul_mx(out=g_turned[:], lhsT=xg[:].bitcast(FP8X4), lhsT_scale=xg_plane[:],
                            rhs=wg[:].bitcast(FP8X4), rhs_scale=wg_plane[:], start=True, stop=True)
        for r in range(PACK):
            xq_pass(r, 1)
        half_g_turned = sbuf("half_g_turned", [P, N], F32)
        nc.scalar.activation(out=half_g_turned[:].rearrange("b (r p) -> b r p", r=PACK),
                             in_=g_turned[:].rearrange("b (p r) -> b r p", r=PACK), func=ACT.Copy, scale=0.5)
        half_g = psum.tile([P, PACK, B], F32, name="half_g", tag="bank1")
        for r in range(PACK):
            nc.tensor.transpose(half_g[:, r, :], half_g_turned[:, r * P:(r + 1) * P], identity[:])

        y = sbuf("y", [P, PACK, B], F32)
        out_rows = out_0.rearrange("(p r) b -> p r b", r=PACK)
        low, high, every = slice(0, B_HALF), slice(B_HALF, B), slice(0, B)

        def combine(r, groups):
            nc.vector.scalar_tensor_tensor(out=y[:, r, groups], in0=peak[:, r, groups], scalar=minus_mean[:, r:r + 1],
                                           in1=half_g[:, r, groups], op0=ALU.add, op1=ALU.add)

        take_peaks(0, 1)
        take_sum(1, 1)
        take_peaks(2, 1)
        take_sum(0, 1)
        take_peaks(1, 1)
        take_sum(3, 1)
        combine(0, every)
        combine(1, every)
        nc.sync.dma_start(out=out_rows[:, 0:2, :], in_=y[:, 0:2, :])
        combine(3, low)
        take_peaks(3, 1)
        take_sum(2, 1)
        combine(2, every)
        combine(3, high)
        nc.sync.dma_start(out=out_rows[:, 2:PACK, :], in_=y[:, 2:PACK, :])

        y_bf = sbuf("y_bf", [P, B, PACK], BF16)
        y_codes = sbuf("y_codes", [P, B], I32)
        y_plane = sbuf("y_plane", [P, B], U8)
        for groups in (low, high):
            nc.vector.tensor_copy(out=y_bf[:, groups, :].rearrange("p (a i) r -> p a r i", i=4),
                                  in_=y[:, :, groups].rearrange("p r (a i) -> p a r i", i=4))
        for groups in (low, high):
            nc.vector.quantize_mx(out=y_codes[:, groups].bitcast(FP8X4), scales=y_plane[:, groups],
                                  in_=y_bf[:, groups, :].rearrange("p b r -> p (b r)"))

        nc.sync.dma_start(out=out_1[0].rearrange("p b r -> p (b r)").bitcast(I32), in_=y_codes[:])
        for q, queue in enumerate((nc.scalar, nc.sync, nc.scalar, nc.sync)):
            queue.dma_start(out=out_2[0, PACK * q:PACK * (q + 1), :].bitcast(I32),
                            in_=y_plane[QUADRANT * q:QUADRANT * q + PACK, :].bitcast(I32))
